import numpy as np
import ml_dtypes


def mxq(x, axis, fmt="e4m3"):
    dtype, down = {"e4m3": (ml_dtypes.float8_e4m3fn, 7), "e5m2": (ml_dtypes.float8_e5m2, 14)}[fmt]
    v = np.moveaxis(np.asarray(x, np.float32).astype(ml_dtypes.bfloat16).astype(np.float64), axis, -1)
    blocks = v.reshape(v.shape[:-1] + (-1, 32))
    amax = np.abs(blocks).max(-1, keepdims=True)
    byte = np.maximum(np.where(amax > 0, np.frexp(amax)[1] - 1 + 127, 0) - down, 1)
    scale = np.exp2(byte - 127.0)
    codes = (blocks / scale).astype(np.float32).astype(dtype).astype(np.float64)
    return np.moveaxis((codes * scale).reshape(v.shape), -1, axis)


WIDE = False


def mx_kscale(k, group=512):
    if not WIDE:
        return np.ones(k)
    levels = np.array([10, -10, 5, -5, 0])
    if group != 512:
        return np.exp2(np.random.permutation(np.resize(levels, k // group))).repeat(group)
    if k % 512:
        return np.exp2(np.random.permutation(np.resize(levels, k // 32))).repeat(32)
    a = np.empty((k // 512, 16))
    for p in range(k // 512):
        a[p, :8] = np.random.permutation(np.resize(levels, 8))
        for g in range(8):
            far = levels[np.abs(levels - a[p, g]) >= 10]
            a[p, g + 8] = far[np.random.randint(len(far))]
    return np.exp2(a.ravel()).repeat(32)


def f64(x):
    return np.asarray(x).astype(np.float64)


def gelu(v):
    return 0.5 * v * (1.0 + np.tanh(0.7978845608028654 * (v + 0.044715 * v ** 3)))


G, D, M, N = 2, 256, 128, 512


def setup_inputs():
    n = np.random.standard_normal
    s = mx_kscale(D, 0)[:, None]
    return {
        "x": (n((G, D, N)) * s).astype(np.float32),
        "w": (n((G, D, M)) / np.sqrt(D) / s).astype(np.float32),
        "u": (n((G, D, M)) / np.sqrt(D) / s).astype(np.float32),
        "b": (0.5 * n((G, M, 1))).astype(np.float32),
        "r": n((G, M, N)).astype(np.float32),
    }


def reference(x, w, u, b, r):
    xq = mxq(f64(x), 1, "e4m3")
    h = mxq(f64(w), 1, "e4m3").transpose(0, 2, 1) @ xq
    g = mxq(f64(u), 1, "e4m3").transpose(0, 2, 1) @ xq
    h = h + f64(b)
    y = gelu(h) * g
    y = y + f64(r)
    return y

@@ -1,0 +1,118 @@
+from contextlib import ExitStack
+
+import concourse.mybir as mybir
+
+G, D, M, N = 2, 256, 128, 512
+FLOPS = 2 * 2 * G * D * M * N
+F32 = mybir.dt.float32
+BF16 = mybir.dt.bfloat16
+U32 = mybir.dt.uint32
+U8 = mybir.dt.uint8
+FP8X4 = mybir.dt.float8_e4m3fn_x4
+GELU = mybir.ActivationFunctionType.Gelu_apprx_tanh
+ALU = mybir.AluOpType
+P = 128
+PACK = 4
+ROWS = 64
+CH = 128
+LOADS = ["w","b","x0","u","x1","x2","x3","r0","r1"]
+SPLIT = {"w":0,"u":0,"x0":128,"x1":48,"x2":48,"x3":48}
+ADDS = [[[0],[0,1]],[[1],[0,1]],[[0,1],[2]],[[0,1],[3]]]
+STORE_Q = "yyyy"
+ORDER = ["cvw","t","qw","csx0","cvu","qx0","h00","h01","csx1","cvx1","qu","g00","g01","qx1","h10","h11","g10","g11","csx2","cvx2","a00","a01","qx2","h20","h21","g20","g21","cvx3","csx3","a10","a11","m00","m01","qx3","h30","h31","g30","g31","a20","a21","m10","m11","p0","s0","m20","m21","p1","s1","a30","a31","m30","m31","p2","s2","p3","s3"]
+ILV = 4
+
+
+def tile_rows_gglu_gelu_bias_res_kernel(tc, x, w, u, b, r, out):
+    nc = tc.nc
+    with ExitStack() as ctx:
+        sb = ctx.enter_context(tc.tile_pool(name="sb", bufs=1))
+        ps = ctx.enter_context(tc.psum_pool(name="ps", bufs=1))
+        ctx.enter_context(tc.manual_schedule())
+        names = ["w", "u", "x0", "x1", "x2", "x3"]
+        src = {"w": w, "u": u}
+        for c in range(4):
+            src["x%d" % c] = x[:, :, c * CH:(c + 1) * CH]
+        raw, grp, codes, scales = {}, {}, {}, {}
+        for k in names:
+            raw[k] = sb.tile([P, PACK, CH], F32, name="raw_" + k, align_bytes=64)
+            grp[k] = sb.tile([P, CH, PACK], BF16, name="grp_" + k, align_bytes=64)
+            codes[k] = sb.tile([P, CH], U32, name="codes_" + k, align_bytes=64)
+            scales[k] = sb.tile([P, CH], U8, name="scales_" + k, align_bytes=64)
+        res = sb.tile([P, G, N], F32, name="res", align_bytes=64)
+        act = sb.tile([P, G, N], F32, name="act", align_bytes=64)
+        prod = sb.tile([P, G, N], F32, name="prod", align_bytes=64)
+        brow = sb.tile([P, G, 32], F32, name="brow", align_bytes=64)
+        bcol = sb.tile([P, G, 32], F32, name="bcol", align_bytes=64)
+        warm = sb.tile([P, 16], F32, name="warm", align_bytes=64)
+        warm2 = sb.tile([P, 16], F32, name="warm2", align_bytes=64)
+        bank = {}
+        for g in range(G):
+            for c in range(4):
+                bank[(g, c)] = ps.tile([P, N], F32, name="bank_%d%d" % (g, c))
+
+        nc.vector.memset(warm[:], 0.0)
+        nc.vector.memset(brow[:], 0.0)
+        nc.scalar.activation(out=warm2[:, 0:1], in_=warm[:, 0:1], func=GELU)
+        for k in LOADS:
+            if k == "b":
+                nc.sync.dma_start(out=brow[0:P:32, :, :], in_=b.rearrange("g (q i) o -> q g (i o)", i=32))
+            elif k[0] == "r":
+                g = int(k[1])
+                nc.sync.dma_start(out=res[:, g, :], in_=r[g])
+            else:
+                nc.sync.dma_start(out=raw[k][:], in_=src[k].rearrange("g (p j) n -> (g p) j n", j=PACK))
+
+        def views(k, lo, hi):
+            dst = grp[k][:, lo:hi, :].rearrange("p (c i) t -> p c t i", i=ILV)
+            srcv = raw[k][:, :, lo:hi].rearrange("p t (c i) -> p c t i", i=ILV)
+            return dst, srcv
+
+        def acc(kind, c, g):
+            off = 0 if kind == "h" else CH
+            return bank[(g, c)][:, off:off + CH]
+
+        for step in ORDER:
+            op = step[0]
+            if op == "t":
+                for g in range(G):
+                    nc.vector.transpose(out=bcol[:, g, :], in_=brow[:, g, :])
+            elif op == "c":
+                k = step[2:]
+                if step[1] == "s":
+                    dst, srcv = views(k, 0, SPLIT[k])
+                    nc.scalar.copy(out=dst, in_=srcv)
+                else:
+                    dst, srcv = views(k, SPLIT[k], CH)
+                    nc.vector.tensor_copy(out=dst, in_=srcv)
+            elif op == "q":
+                k = step[1:]
+                nc.vector.quantize_mx(out=codes[k][:].bitcast(FP8X4), scales=scales[k][:],
+                                      in_=grp[k][:].rearrange("p n j -> p (n j)"))
+            elif op in ("h", "g"):
+                c, g = int(step[1]), int(step[2])
+                k = "w" if op == "h" else "u"
+                rows = slice(ROWS * g, ROWS * (g + 1))
+                xk = "x%d" % c
+                nc.tensor.matmul_mx(out=acc(op, c, g), lhsT=codes[k][rows, :].bitcast(FP8X4),
+                                    lhsT_scale=scales[k][rows, :], rhs=codes[xk][rows, :].bitcast(FP8X4),
+                                    rhs_scale=scales[xk][rows, :], start=True, stop=True)
+            elif op == "a":
+                c, g = int(step[1]), int(step[2])
+                nc.scalar.activation(out=act[:, g, c * CH:(c + 1) * CH], in_=acc("h", c, g), func=GELU,
+                                     bias=bcol[:, g, 0:1])
+            elif op == "m":
+                c, g = int(step[1]), int(step[2])
+                nc.vector.tensor_tensor(out=prod[:, g, c * CH:(c + 1) * CH], in0=acc("g", c, g),
+                                        in1=act[:, g, c * CH:(c + 1) * CH], op=ALU.mult)
+            else:
+                i = int(step[1:])
+                gs, cs = ADDS[i]
+                gsl = slice(gs[0], gs[-1] + 1)
+                csl = slice(cs[0] * CH, (cs[-1] + 1) * CH)
+                if op == "p":
+                    nc.vector.tensor_tensor(out=res[:, gsl, csl], in0=prod[:, gsl, csl], in1=res[:, gsl, csl],
+                                            op=ALU.add)
+                else:
+                    q = nc.sync if STORE_Q[i] == "y" else nc.scalar
+                    q.dma_start(out=out[gsl, :, csl].rearrange("g m n -> m g n"), in_=res[:, gsl, csl])

@@ -15,11 +15,12 @@ P = 128
 PACK = 4
 ROWS = 64
 CH = 128
-LOADS = ["w","b","x0","u","x1","x2","x3","r0","r1"]
-SPLIT = {"w":0,"u":0,"x0":128,"x1":48,"x2":48,"x3":48}
-ADDS = [[[0],[0,1]],[[1],[0,1]],[[0,1],[2]],[[0,1],[3]]]
-STORE_Q = "yyyy"
-ORDER = ["cvw","t","qw","csx0","cvu","qx0","h00","h01","csx1","cvx1","qu","g00","g01","qx1","h10","h11","g10","g11","csx2","cvx2","a00","a01","qx2","h20","h21","g20","g21","cvx3","csx3","a10","a11","m00","m01","qx3","h30","h31","g30","g31","a20","a21","m10","m11","p0","s0","m20","m21","p1","s1","a30","a31","m30","m31","p2","s2","p3","s3"]
+LOADS = ["w","b","x01","u","x2","x3","r0","r1"]
+SPLIT = {"w":48,"u":48,"x0":32,"x1":64,"x2":48,"x3":64}
+ADDS = [[[0],[0,1]],[[1],[0,1]],[[0,1],[2]],[[0],[3]],[[1],[3]]]
+STORE_Q = "yyyyy"
+ORDER = ["cvw","csw","t","qw","cvx0","csx0","csx1","cvx1","qx0","csu","cvu","qx1","h01","h00","qu","h10","csx2","cvx2","g00","a00","h11","g10","a10","qx2","g01","a01","m00","g11","csx3","cvx3","h20","m10","h21","a11","m01","g20","a20","qx3","a21","p0","g21","h30","m11","g30","m20","h31","s0","m21","a30","g31","p1","a31","m30","p2","s1","m31","p3","s2","p4","s3","s4"]
+ACT_LOADS = []
 ILV = 4
 
 
@@ -30,12 +31,8 @@ def tile_rows_gglu_gelu_bias_res_kernel(tc, x, w, u, b, r, out):
         ps = ctx.enter_context(tc.psum_pool(name="ps", bufs=1))
         ctx.enter_context(tc.manual_schedule())
         names = ["w", "u", "x0", "x1", "x2", "x3"]
-        src = {"w": w, "u": u}
-        for c in range(4):
-            src["x%d" % c] = x[:, :, c * CH:(c + 1) * CH]
         raw, grp, codes, scales = {}, {}, {}, {}
         for k in names:
-            raw[k] = sb.tile([P, PACK, CH], F32, name="raw_" + k, align_bytes=64)
             grp[k] = sb.tile([P, CH, PACK], BF16, name="grp_" + k, align_bytes=64)
             codes[k] = sb.tile([P, CH], U32, name="codes_" + k, align_bytes=64)
             scales[k] = sb.tile([P, CH], U8, name="scales_" + k, align_bytes=64)
@@ -47,21 +44,36 @@ def tile_rows_gglu_gelu_bias_res_kernel(tc, x, w, u, b, r, out):
         warm = sb.tile([P, 16], F32, name="warm", align_bytes=64)
         warm2 = sb.tile([P, 16], F32, name="warm2", align_bytes=64)
         bank = {}
-        for g in range(G):
-            for c in range(4):
-                bank[(g, c)] = ps.tile([P, N], F32, name="bank_%d%d" % (g, c))
+        for kind in ("h", "g"):
+            for g in range(G):
+                for par in range(2):
+                    bank[(kind, g, par)] = ps.tile([P, N], F32, name="bank_%s%d%d" % (kind, g, par))
 
-        nc.vector.memset(warm[:], 0.0)
         nc.vector.memset(brow[:], 0.0)
-        nc.scalar.activation(out=warm2[:, 0:1], in_=warm[:, 0:1], func=GELU)
+        nc.vector.memset(warm[:], 0.0)
         for k in LOADS:
+            eng = nc.scalar if k in ACT_LOADS else nc.sync
             if k == "b":
-                nc.sync.dma_start(out=brow[0:P:32, :, :], in_=b.rearrange("g (q i) o -> q g (i o)", i=32))
+                eng.dma_start(out=brow[0:P:32, :, :], in_=b.rearrange("g (q i) o -> q g (i o)", i=32))
             elif k[0] == "r":
                 g = int(k[1])
-                nc.sync.dma_start(out=res[:, g, :], in_=r[g])
+                eng.dma_start(out=res[:, g, :], in_=r[g])
+            elif k[0] == "R":
+                cols = slice(int(k[1]) * CH, (int(k[-1]) + 1) * CH)
+                eng.dma_start(out=res[:, :, cols], in_=r[:, :, cols].rearrange("g m n -> m g n"))
             else:
-                nc.sync.dma_start(out=raw[k][:], in_=src[k].rearrange("g (p j) n -> (g p) j n", j=PACK))
+                if k[0] == "x":
+                    c0, c1 = int(k[1]), int(k[-1]) + 1
+                    dram = x[:, :, c0 * CH:c1 * CH]
+                    parts = ["x%d" % c for c in range(c0, c1)]
+                else:
+                    dram = w if k == "w" else u
+                    parts = [k]
+                t = sb.tile([P, PACK, CH * len(parts)], F32, name="raw_" + k, align_bytes=64)
+                eng.dma_start(out=t[:], in_=dram.rearrange("g (p j) n -> (g p) j n", j=PACK))
+                for i, part in enumerate(parts):
+                    raw[part] = t[:, :, i * CH:(i + 1) * CH]
+        nc.scalar.activation(out=warm2[:, 0:1], in_=warm[:, 0:1], func=GELU)
 
         def views(k, lo, hi):
             dst = grp[k][:, lo:hi, :].rearrange("p (c i) t -> p c t i", i=ILV)
@@ -69,8 +81,7 @@ def tile_rows_gglu_gelu_bias_res_kernel(tc, x, w, u, b, r, out):
             return dst, srcv
 
         def acc(kind, c, g):
-            off = 0 if kind == "h" else CH
-            return bank[(g, c)][:, off:off + CH]
+            return bank[(kind, g, c % 2)][:, (c // 2) * CH:(c // 2 + 1) * CH]
 
         for step in ORDER:
             op = step[0]

@@ -15,12 +15,13 @@ P = 128
 PACK = 4
 ROWS = 64
 CH = 128
-LOADS = ["w","b","x01","u","x2","x3","r0","r1"]
-SPLIT = {"w":48,"u":48,"x0":32,"x1":64,"x2":48,"x3":64}
-ADDS = [[[0],[0,1]],[[1],[0,1]],[[0,1],[2]],[[0],[3]],[[1],[3]]]
-STORE_Q = "yyyyy"
-ORDER = ["cvw","csw","t","qw","cvx0","csx0","csx1","cvx1","qx0","csu","cvu","qx1","h01","h00","qu","h10","csx2","cvx2","g00","a00","h11","g10","a10","qx2","g01","a01","m00","g11","csx3","cvx3","h20","m10","h21","a11","m01","g20","a20","qx3","a21","p0","g21","h30","m11","g30","m20","h31","s0","m21","a30","g31","p1","a31","m30","p2","s1","m31","p3","s2","p4","s3","s4"]
+LOADS = ["w","b","x0","u","x1","x2","x3","r0","r1"]
+SPLIT = {"w":0,"u":128,"x0":32,"x1":0,"x2":32,"x3":48}
+ADDS = [[[0],[0,1]],[[1],[0,1]],[[0,1],[2]],[[0,1],[3]]]
+STORE_Q = "yyyy"
+ORDER = ["cvw","csx0","cvx0","qw","t","csu","qx0","h00","h01","cvx1","qu","g00","g01","csx2","qx1","h10","h11","g10","g11","cvx2","csx3","cvx3","qx2","h20","h21","g20","g21","qx3","h30","h31","g30","g31","a00","a10","a01","a11","m00","m10","m01","m11","a20","a21","a30","a31","p0","p1","s0","s1","m20","m21","m30","m31","p2","p3","s2","s3"]
 ACT_LOADS = []
+ADD_E = "VGVV"
 ILV = 4
 
 
@@ -44,10 +45,9 @@ def tile_rows_gglu_gelu_bias_res_kernel(tc, x, w, u, b, r, out):
         warm = sb.tile([P, 16], F32, name="warm", align_bytes=64)
         warm2 = sb.tile([P, 16], F32, name="warm2", align_bytes=64)
         bank = {}
-        for kind in ("h", "g"):
-            for g in range(G):
-                for par in range(2):
-                    bank[(kind, g, par)] = ps.tile([P, N], F32, name="bank_%s%d%d" % (kind, g, par))
+        for g in range(G):
+            for c in range(4):
+                bank[(g, c)] = ps.tile([P, N], F32, name="bank_%d%d" % (g, c))
 
         nc.vector.memset(brow[:], 0.0)
         nc.vector.memset(warm[:], 0.0)
@@ -81,7 +81,8 @@ def tile_rows_gglu_gelu_bias_res_kernel(tc, x, w, u, b, r, out):
             return dst, srcv
 
         def acc(kind, c, g):
-            return bank[(kind, g, c % 2)][:, (c // 2) * CH:(c // 2 + 1) * CH]
+            off = 0 if kind == "h" else CH
+            return bank[(g, c)][:, off:off + CH]
 
         for step in ORDER:
             op = step[0]
@@ -122,7 +123,8 @@ def tile_rows_gglu_gelu_bias_res_kernel(tc, x, w, u, b, r, out):
                 gsl = slice(gs[0], gs[-1] + 1)
                 csl = slice(cs[0] * CH, (cs[-1] + 1) * CH)
                 if op == "p":
-                    nc.vector.tensor_tensor(out=res[:, gsl, csl], in0=prod[:, gsl, csl], in1=res[:, gsl, csl],
+                    adder = nc.gpsimd if ADD_E[i] == "G" else nc.vector
+                    adder.tensor_tensor(out=res[:, gsl, csl], in0=prod[:, gsl, csl], in1=res[:, gsl, csl],
                                             op=ALU.add)
                 else:
                     q = nc.sync if STORE_Q[i] == "y" else nc.scalar

@@ -15,13 +15,13 @@ P = 128
 PACK = 4
 ROWS = 64
 CH = 128
-LOADS = ["w","b","x0","u","x1","x2","x3","r0","r1"]
-SPLIT = {"w":0,"u":128,"x0":32,"x1":0,"x2":32,"x3":48}
-ADDS = [[[0],[0,1]],[[1],[0,1]],[[0,1],[2]],[[0,1],[3]]]
-STORE_Q = "yyyy"
-ORDER = ["cvw","csx0","cvx0","qw","t","csu","qx0","h00","h01","cvx1","qu","g00","g01","csx2","qx1","h10","h11","g10","g11","cvx2","csx3","cvx3","qx2","h20","h21","g20","g21","qx3","h30","h31","g30","g31","a00","a10","a01","a11","m00","m10","m01","m11","a20","a21","a30","a31","p0","p1","s0","s1","m20","m21","m30","m31","p2","p3","s2","s3"]
+LOADS = ["w","b","x0","u","x1","x2","x3","R01","R23"]
+SPLIT = {"w":0,"u":0,"x0":128,"x1":128,"x2":0,"x3":48}
+ADDS = [[[0,1],[0]],[[0,1],[1]],[[0,1],[2]],[[0],[3]],[[1],[3]]]
+STORE_Q = "yyyyy"
+ORDER = ["cvw","t","csx0","qw","cvu","qx0","h00","h01","qu","g00","g01","csx1","cvx2","a00","a01","qx1","h10","h11","g10","g11","qx2","h20","h21","g20","g21","csx3","cvx3","m00","m01","qx3","h30","h31","g30","g31","a10","a11","p0","s0","a20","a21","m10","m11","m20","m21","a30","a31","p1","s1","m30","p2","s2","m31","p3","s3","p4","s4"]
 ACT_LOADS = []
-ADD_E = "VGVV"
+ADD_E = "VVVVV"
 ILV = 4
 
 

from contextlib import ExitStack

import concourse.mybir as mybir

G, D, M, N = 2, 256, 128, 512
FLOPS = 2 * 2 * G * D * M * N
F32 = mybir.dt.float32
BF16 = mybir.dt.bfloat16
U32 = mybir.dt.uint32
U8 = mybir.dt.uint8
FP8X4 = mybir.dt.float8_e4m3fn_x4
GELU = mybir.ActivationFunctionType.Gelu_apprx_tanh
ALU = mybir.AluOpType
P = 128
PACK = 4
ROWS = 64
CH = 128
LOADS = ["w","b","x0","u","x1","x2","x3","R01","R23"]
SPLIT = {"w":0,"u":0,"x0":128,"x1":128,"x2":0,"x3":48}
ADDS = [[[0,1],[0]],[[0,1],[1]],[[0,1],[2]],[[0],[3]],[[1],[3]]]
STORE_Q = "yyyyy"
ORDER = ["cvw","t","csx0","qw","cvu","qx0","h00","h01","qu","g00","g01","csx1","cvx2","a00","a01","qx1","h10","h11","g10","g11","qx2","h20","h21","g20","g21","csx3","cvx3","m00","m01","qx3","h30","h31","g30","g31","a10","a11","p0","s0","a20","a21","m10","m11","m20","m21","a30","a31","p1","s1","m30","p2","s2","m31","p3","s3","p4","s4"]
ACT_LOADS = []
ADD_E = "VVVVV"
ILV = 4


def tile_rows_gglu_gelu_bias_res_kernel(tc, x, w, u, b, r, out):
    nc = tc.nc
    with ExitStack() as ctx:
        sb = ctx.enter_context(tc.tile_pool(name="sb", bufs=1))
        ps = ctx.enter_context(tc.psum_pool(name="ps", bufs=1))
        ctx.enter_context(tc.manual_schedule())
        names = ["w", "u", "x0", "x1", "x2", "x3"]
        raw, grp, codes, scales = {}, {}, {}, {}
        for k in names:
            grp[k] = sb.tile([P, CH, PACK], BF16, name="grp_" + k, align_bytes=64)
            codes[k] = sb.tile([P, CH], U32, name="codes_" + k, align_bytes=64)
            scales[k] = sb.tile([P, CH], U8, name="scales_" + k, align_bytes=64)
        res = sb.tile([P, G, N], F32, name="res", align_bytes=64)
        act = sb.tile([P, G, N], F32, name="act", align_bytes=64)
        prod = sb.tile([P, G, N], F32, name="prod", align_bytes=64)
        brow = sb.tile([P, G, 32], F32, name="brow", align_bytes=64)
        bcol = sb.tile([P, G, 32], F32, name="bcol", align_bytes=64)
        warm = sb.tile([P, 16], F32, name="warm", align_bytes=64)
        warm2 = sb.tile([P, 16], F32, name="warm2", align_bytes=64)
        bank = {}
        for g in range(G):
            for c in range(4):
                bank[(g, c)] = ps.tile([P, N], F32, name="bank_%d%d" % (g, c))

        nc.vector.memset(brow[:], 0.0)
        nc.vector.memset(warm[:], 0.0)
        for k in LOADS:
            eng = nc.scalar if k in ACT_LOADS else nc.sync
            if k == "b":
                eng.dma_start(out=brow[0:P:32, :, :], in_=b.rearrange("g (q i) o -> q g (i o)", i=32))
            elif k[0] == "r":
                g = int(k[1])
                eng.dma_start(out=res[:, g, :], in_=r[g])
            elif k[0] == "R":
                cols = slice(int(k[1]) * CH, (int(k[-1]) + 1) * CH)
                eng.dma_start(out=res[:, :, cols], in_=r[:, :, cols].rearrange("g m n -> m g n"))
            else:
                if k[0] == "x":
                    c0, c1 = int(k[1]), int(k[-1]) + 1
                    dram = x[:, :, c0 * CH:c1 * CH]
                    parts = ["x%d" % c for c in range(c0, c1)]
                else:
                    dram = w if k == "w" else u
                    parts = [k]
                t = sb.tile([P, PACK, CH * len(parts)], F32, name="raw_" + k, align_bytes=64)
                eng.dma_start(out=t[:], in_=dram.rearrange("g (p j) n -> (g p) j n", j=PACK))
                for i, part in enumerate(parts):
                    raw[part] = t[:, :, i * CH:(i + 1) * CH]
        nc.scalar.activation(out=warm2[:, 0:1], in_=warm[:, 0:1], func=GELU)

        def views(k, lo, hi):
            dst = grp[k][:, lo:hi, :].rearrange("p (c i) t -> p c t i", i=ILV)
            srcv = raw[k][:, :, lo:hi].rearrange("p t (c i) -> p c t i", i=ILV)
            return dst, srcv

        def acc(kind, c, g):
            off = 0 if kind == "h" else CH
            return bank[(g, c)][:, off:off + CH]

        for step in ORDER:
            op = step[0]
            if op == "t":
                for g in range(G):
                    nc.vector.transpose(out=bcol[:, g, :], in_=brow[:, g, :])
            elif op == "c":
                k = step[2:]
                if step[1] == "s":
                    dst, srcv = views(k, 0, SPLIT[k])
                    nc.scalar.copy(out=dst, in_=srcv)
                else:
                    dst, srcv = views(k, SPLIT[k], CH)
                    nc.vector.tensor_copy(out=dst, in_=srcv)
            elif op == "q":
                k = step[1:]
                nc.vector.quantize_mx(out=codes[k][:].bitcast(FP8X4), scales=scales[k][:],
                                      in_=grp[k][:].rearrange("p n j -> p (n j)"))
            elif op in ("h", "g"):
                c, g = int(step[1]), int(step[2])
                k = "w" if op == "h" else "u"
                rows = slice(ROWS * g, ROWS * (g + 1))
                xk = "x%d" % c
                nc.tensor.matmul_mx(out=acc(op, c, g), lhsT=codes[k][rows, :].bitcast(FP8X4),
                                    lhsT_scale=scales[k][rows, :], rhs=codes[xk][rows, :].bitcast(FP8X4),
                                    rhs_scale=scales[xk][rows, :], start=True, stop=True)
            elif op == "a":
                c, g = int(step[1]), int(step[2])
                nc.scalar.activation(out=act[:, g, c * CH:(c + 1) * CH], in_=acc("h", c, g), func=GELU,
                                     bias=bcol[:, g, 0:1])
            elif op == "m":
                c, g = int(step[1]), int(step[2])
                nc.vector.tensor_tensor(out=prod[:, g, c * CH:(c + 1) * CH], in0=acc("g", c, g),
                                        in1=act[:, g, c * CH:(c + 1) * CH], op=ALU.mult)
            else:
                i = int(step[1:])
                gs, cs = ADDS[i]
                gsl = slice(gs[0], gs[-1] + 1)
                csl = slice(cs[0] * CH, (cs[-1] + 1) * CH)
                if op == "p":
                    adder = nc.gpsimd if ADD_E[i] == "G" else nc.vector
                    adder.tensor_tensor(out=res[:, gsl, csl], in0=prod[:, gsl, csl], in1=res[:, gsl, csl],
                                            op=ALU.add)
                else:
                    q = nc.sync if STORE_Q[i] == "y" else nc.scalar
                    q.dma_start(out=out[gsl, :, csl].rearrange("g m n -> m g n"), in_=res[:, gsl, csl])
